import numpy as np
import ml_dtypes


def mxq(x, axis, fmt="e4m3"):
    dtype, down = {"e4m3": (ml_dtypes.float8_e4m3fn, 7), "e5m2": (ml_dtypes.float8_e5m2, 14)}[fmt]
    v = np.moveaxis(np.asarray(x, np.float32).astype(ml_dtypes.bfloat16).astype(np.float64), axis, -1)
    blocks = v.reshape(v.shape[:-1] + (-1, 32))
    amax = np.abs(blocks).max(-1, keepdims=True)
    byte = np.maximum(np.where(amax > 0, np.frexp(amax)[1] - 1 + 127, 0) - down, 1)
    scale = np.exp2(byte - 127.0)
    codes = (blocks / scale).astype(np.float32).astype(dtype).astype(np.float64)
    return np.moveaxis((codes * scale).reshape(v.shape), -1, axis)


WIDE = False


def mx_kscale(k):
    if not WIDE:
        return np.ones(k)
    levels = np.array([10, -10, 5, -5, 0])
    if k % 512:
        return np.exp2(np.random.permutation(np.resize(levels, k // 32))).repeat(32)
    a = np.empty((k // 512, 16))
    for p in range(k // 512):
        a[p, :8] = np.random.permutation(np.resize(levels, 8))
        for g in range(8):
            far = levels[np.abs(levels - a[p, g]) >= 10]
            a[p, g + 8] = far[np.random.randint(len(far))]
    return np.exp2(a.ravel()).repeat(32)


def f64(x):
    return np.asarray(x).astype(np.float64)


def striped8(idx):
    return np.concatenate([x.reshape(-1, 16).T for x in idx]).astype(np.uint16)


def runs(offs, k):
    lists = np.stack([offs[16 * r : 16 * r + 16].T.reshape(-1) for r in range(8)]).astype(np.int64)
    return lists[np.arange(k) % 512 // 64]


def pack_weight(w):
    k, n = w.shape
    w = f64(np.asarray(w, np.float32).astype(ml_dtypes.bfloat16)).reshape(k // 32, 32, n)
    amax = np.abs(w).max(1)
    byte = np.clip(np.where(amax > 0, np.frexp(amax)[1] - 1 + 127 - 7, 1), 1, 254)
    scaled = (w * np.exp2(127.0 - byte)[:, None, :]).reshape(k, n).astype(np.float32)
    words = np.ascontiguousarray(scaled.reshape(k // 512, 128, 4, n).transpose(0, 1, 3, 2)).astype(ml_dtypes.float8_e4m3fn).view(np.uint8)
    return words, np.ascontiguousarray(byte.astype(np.uint8).reshape(k // 512, 16, n))


def unpack_weight(words, scales):
    g, p, n, _ = words.shape
    vals = np.ascontiguousarray(words).view(ml_dtypes.float8_e4m3fn).astype(np.float64) * np.repeat(np.exp2(scales.astype(np.float64) - 127.0), 8, axis=1)[..., None]
    return vals.transpose(0, 1, 3, 2).reshape(g * 512, n)


K, T, S, H, N, V = 512, 2048, 1024, 512, 128, 512


def setup_inputs():
    n = np.random.standard_normal
    s = mx_kscale(K)[:, None]
    u = mx_kscale(H)
    packed_xT = pack_weight(n((K, T)) * s)
    return {
        "x_words": packed_xT[0],
        "x_scales": packed_xT[1],
        "w1": (n((K, H)) / np.sqrt(K) / s * u).astype(np.float32),
        "w2": (n((H, N)) / np.sqrt(H) / u[:, None]).astype(np.float32),
        "offs": striped8(np.stack([np.random.permutation(T)[:S] for _ in range(8)])),
    }


def reference(x_words, x_scales, w1, w2, offs):
    xq = unpack_weight(x_words, x_scales)[np.arange(K)[:, None], runs(offs, K)]
    y = mxq(f64(w1), 0, "e4m3").T @ xq
    z = np.maximum(y[:, :V], y[:, V:2 * V])
    return mxq(f64(w2), 0, "e4m3").T @ mxq(z, 0, "e4m3")

@@ -1,0 +1,143 @@
+from contextlib import ExitStack
+
+import concourse.mybir as mybir
+
+K, T, S, H, N, V = 512, 2048, 1024, 512, 128, 512
+FLOPS = 2 * K * H * S + 2 * H * N * V
+
+F32 = mybir.dt.float32
+BF16 = mybir.dt.bfloat16
+I32 = mybir.dt.int32
+U32 = mybir.dt.uint32
+U16 = mybir.dt.uint16
+U8 = mybir.dt.uint8
+FP8X4 = mybir.dt.float8_e4m3fn_x4
+MAX = mybir.AluOpType.max
+
+P = 128
+PACK = 4
+PIECE = 256
+BLOCK = 128
+W1_CHUNKS = [(0, 256), (256, 384), (384, 512)]
+
+
+def tile_picked_phpool_none_p_kernel(tc, x_words, x_scales, w1, w2, offs, out):
+    nc = tc.nc
+    with ExitStack() as ctx:
+        keep = ctx.enter_context(tc.tile_pool(name="keep", bufs=1))
+        ring = ctx.enter_context(tc.tile_pool(name="ring", bufs=4))
+        psum_a = ctx.enter_context(tc.psum_pool(name="psum_a", bufs=3))
+        psum_b = ctx.enter_context(tc.psum_pool(name="psum_b", bufs=3))
+        psum_o = ctx.enter_context(tc.psum_pool(name="psum_o", bufs=2))
+
+        offsets = keep.tile([P, S // 16], U16, name="offsets")
+        nc.sync.dma_start(offsets[:], offs)
+
+        scale_table = keep.tile([P, T], U8, name="scale_table", align_bytes=64)
+        nc.vector.memset(scale_table[:].bitcast(I32), 0)
+        nc.scalar.dma_start(scale_table[0:P:8, :].bitcast(I32), x_scales[0].bitcast(I32))
+        x_plane = keep.tile([P, S], U8, name="x_plane", align_bytes=64)
+        nc.vector.memset(x_plane[:].bitcast(I32), 0)
+
+        word_table = keep.tile([P, T], I32, name="word_table", align_bytes=64)
+        nc.sync.dma_start(word_table[:], x_words[0].rearrange("p n t -> p (n t)").bitcast(I32))
+
+        w1_rows = w1.rearrange("(p j) c -> p j c", j=PACK)
+        w1_raw = []
+        for n, (c0, c1) in enumerate(W1_CHUNKS):
+            raw = keep.tile([P, PACK, c1 - c0], F32, name="w1_raw%d" % n)
+            nc.sync.dma_start(raw[:], w1_rows[:, :, c0:c1])
+            w1_raw.append(raw)
+        w2_raw = keep.tile([P, PACK, N], F32, name="w2_raw")
+        nc.sync.dma_start(w2_raw[:], w2.rearrange("(p j) n -> p j n", j=PACK))
+
+        picked_scales = keep.tile([P, S], U8, name="picked_scales", align_bytes=64)
+        nc.vector.tensor_copy(picked_scales[:], scale_table[:].indirect(offsets[:]))
+        for j in range(4):
+            nc.sync.dma_start(
+                x_plane[j:P:32, :].bitcast(I32), picked_scales[8 * j : P : 32, :].bitcast(I32)
+            )
+
+        picked_words = {}
+        for half in range(V // PIECE):
+            for read in range(2):
+                first = read * V + half * PIECE
+                words = keep.tile([P, PIECE], U32, name="picked_words%d" % first, align_bytes=64)
+                nc.vector.tensor_copy(
+                    words[:],
+                    word_table[:].bitcast(U32).indirect(offsets[:, first // 16 : (first + PIECE) // 16]),
+                )
+                picked_words[first] = words
+
+        w1_bf = keep.tile([P, PACK, P, PACK], BF16, name="w1_bf", align_bytes=64)
+        for raw, (c0, c1) in zip(w1_raw, W1_CHUNKS):
+            nc.scalar.copy(
+                w1_bf[:, :, c0 // PACK : c1 // PACK, :].rearrange("p t m j -> p m t j"),
+                raw[:].rearrange("p j (m t) -> p m t j", t=PACK),
+            )
+        w1_codes, w1_plane = [], []
+        for t in range(PACK):
+            codes = keep.tile([P, P], U32, name="w1_codes%d" % t, align_bytes=64)
+            plane = keep.tile([P, P], U8, name="w1_plane%d" % t, align_bytes=64)
+            nc.vector.quantize_mx(
+                out=codes[:].bitcast(FP8X4), scales=plane[:], in_=w1_bf[:, t].rearrange("p m j -> p (m j)")
+            )
+            w1_codes.append(codes)
+            w1_plane.append(plane)
+
+        w2_bf = keep.tile([P, N, PACK], BF16, name="w2_bf", align_bytes=64)
+        nc.scalar.copy(w2_bf[:], w2_raw[:].rearrange("p j n -> p n j"))
+        w2_codes = keep.tile([P, N], U32, name="w2_codes", align_bytes=64)
+        w2_plane = keep.tile([P, N], U8, name="w2_plane", align_bytes=64)
+        nc.vector.quantize_mx(
+            out=w2_codes[:].bitcast(FP8X4), scales=w2_plane[:], in_=w2_bf[:].rearrange("p n j -> p (n j)")
+        )
+
+        def project(bank, first):
+            words = picked_words[first // PIECE * PIECE]
+            inside = first % PIECE
+            for t in range(PACK):
+                nc.tensor.matmul_mx(
+                    out=bank[:, t, :],
+                    lhsT=w1_codes[t][:].bitcast(FP8X4),
+                    lhsT_scale=w1_plane[t][:],
+                    rhs=words[:, inside : inside + BLOCK].bitcast(FP8X4),
+                    rhs_scale=x_plane[:, first : first + BLOCK],
+                    start=True,
+                    stop=True,
+                )
+
+        def second_layer(v0, z_bf):
+            z_codes = ring.tile([P, BLOCK], U32, name="z_codes", align_bytes=64)
+            z_plane = ring.tile([P, BLOCK], U8, name="z_plane", align_bytes=64)
+            nc.vector.quantize_mx(
+                out=z_codes[:].bitcast(FP8X4), scales=z_plane[:], in_=z_bf[:].rearrange("p v t -> p (v t)")
+            )
+            bank_o = psum_o.tile([P, BLOCK], F32, name="bank_o")
+            nc.tensor.matmul_mx(
+                out=bank_o[:],
+                lhsT=w2_codes[:].bitcast(FP8X4),
+                lhsT_scale=w2_plane[:],
+                rhs=z_codes[:].bitcast(FP8X4),
+                rhs_scale=z_plane[:],
+                start=True,
+                stop=True,
+            )
+            result = ring.tile([P, BLOCK], F32, name="result")
+            nc.scalar.copy(result[:], bank_o[:])
+            nc.sync.dma_start(out[:, v0 : v0 + BLOCK], result[:])
+
+        waiting = None
+        for v0 in range(0, V, BLOCK):
+            bank_a = psum_a.tile([P, PACK, BLOCK], F32, name="bank_a")
+            bank_b = psum_b.tile([P, PACK, BLOCK], F32, name="bank_b")
+            project(bank_a, v0)
+            project(bank_b, V + v0)
+            first_read = ring.tile([P, BLOCK, PACK], F32, name="first_read")
+            nc.scalar.copy(first_read[:], bank_a[:].rearrange("p t v -> p v t"))
+            z_bf = ring.tile([P, BLOCK, PACK], BF16, name="z_bf", align_bytes=64)
+            nc.vector.tensor_tensor(z_bf[:], bank_b[:].rearrange("p t v -> p v t"), first_read[:], MAX)
+            if waiting is not None:
+                second_layer(*waiting)
+            waiting = (v0, z_bf)
+        second_layer(*waiting)

@@ -18,7 +18,7 @@ P = 128
 PACK = 4
 PIECE = 256
 BLOCK = 128
-W1_CHUNKS = [(0, 256), (256, 384), (384, 512)]
+W1_CHUNKS = [(0, 128), (128, 384), (384, 512)]
 
 
 def tile_picked_phpool_none_p_kernel(tc, x_words, x_scales, w1, w2, offs, out):
@@ -35,12 +35,10 @@ def tile_picked_phpool_none_p_kernel(tc, x_words, x_scales, w1, w2, offs, out):
 
         scale_table = keep.tile([P, T], U8, name="scale_table", align_bytes=64)
         nc.vector.memset(scale_table[:].bitcast(I32), 0)
-        nc.scalar.dma_start(scale_table[0:P:8, :].bitcast(I32), x_scales[0].bitcast(I32))
         x_plane = keep.tile([P, S], U8, name="x_plane", align_bytes=64)
         nc.vector.memset(x_plane[:].bitcast(I32), 0)
 
         word_table = keep.tile([P, T], I32, name="word_table", align_bytes=64)
-        nc.sync.dma_start(word_table[:], x_words[0].rearrange("p n t -> p (n t)").bitcast(I32))
 
         w1_rows = w1.rearrange("(p j) c -> p j c", j=PACK)
         w1_raw = []
@@ -48,6 +46,9 @@ def tile_picked_phpool_none_p_kernel(tc, x_words, x_scales, w1, w2, offs, out):
             raw = keep.tile([P, PACK, c1 - c0], F32, name="w1_raw%d" % n)
             nc.sync.dma_start(raw[:], w1_rows[:, :, c0:c1])
             w1_raw.append(raw)
+            if n == 0:
+                nc.sync.dma_start(scale_table[0:P:8, :].bitcast(I32), x_scales[0].bitcast(I32))
+        nc.sync.dma_start(word_table[:], x_words[0].rearrange("p n t -> p (n t)").bitcast(I32))
         w2_raw = keep.tile([P, PACK, N], F32, name="w2_raw")
         nc.sync.dma_start(w2_raw[:], w2.rearrange("(p j) n -> p j n", j=PACK))
 
@@ -57,6 +58,20 @@ def tile_picked_phpool_none_p_kernel(tc, x_words, x_scales, w1, w2, offs, out):
             nc.sync.dma_start(
                 x_plane[j:P:32, :].bitcast(I32), picked_scales[8 * j : P : 32, :].bitcast(I32)
             )
+
+        w1_bf = keep.tile([P, PACK, P, PACK], BF16, name="w1_bf", align_bytes=64)
+        for raw, (c0, c1) in zip(w1_raw, W1_CHUNKS):
+            nc.scalar.copy(
+                w1_bf[:, :, c0 // PACK : c1 // PACK, :].rearrange("p t m j -> p m t j"),
+                raw[:].rearrange("p j (m t) -> p m t j", t=PACK),
+            )
+        w1_codes = keep.tile([P, PACK, P], U32, name="w1_codes", align_bytes=64)
+        w1_plane = keep.tile([P, PACK, P], U8, name="w1_plane", align_bytes=64)
+        nc.vector.quantize_mx(
+            out=w1_codes[:].rearrange("p t m -> p (t m)").bitcast(FP8X4),
+            scales=w1_plane[:].rearrange("p t m -> p (t m)"),
+            in_=w1_bf[:].rearrange("p t m j -> p (t m j)"),
+        )
 
         picked_words = {}
         for half in range(V // PIECE):
@@ -68,22 +83,6 @@ def tile_picked_phpool_none_p_kernel(tc, x_words, x_scales, w1, w2, offs, out):
                     word_table[:].bitcast(U32).indirect(offsets[:, first // 16 : (first + PIECE) // 16]),
                 )
                 picked_words[first] = words
-
-        w1_bf = keep.tile([P, PACK, P, PACK], BF16, name="w1_bf", align_bytes=64)
-        for raw, (c0, c1) in zip(w1_raw, W1_CHUNKS):
-            nc.scalar.copy(
-                w1_bf[:, :, c0 // PACK : c1 // PACK, :].rearrange("p t m j -> p m t j"),
-                raw[:].rearrange("p j (m t) -> p m t j", t=PACK),
-            )
-        w1_codes, w1_plane = [], []
-        for t in range(PACK):
-            codes = keep.tile([P, P], U32, name="w1_codes%d" % t, align_bytes=64)
-            plane = keep.tile([P, P], U8, name="w1_plane%d" % t, align_bytes=64)
-            nc.vector.quantize_mx(
-                out=codes[:].bitcast(FP8X4), scales=plane[:], in_=w1_bf[:, t].rearrange("p m j -> p (m j)")
-            )
-            w1_codes.append(codes)
-            w1_plane.append(plane)
 
         w2_bf = keep.tile([P, N, PACK], BF16, name="w2_bf", align_bytes=64)
         nc.scalar.copy(w2_bf[:], w2_raw[:].rearrange("p j n -> p n j"))
@@ -99,8 +98,8 @@ def tile_picked_phpool_none_p_kernel(tc, x_words, x_scales, w1, w2, offs, out):
             for t in range(PACK):
                 nc.tensor.matmul_mx(
                     out=bank[:, t, :],
-                    lhsT=w1_codes[t][:].bitcast(FP8X4),
-                    lhsT_scale=w1_plane[t][:],
+                    lhsT=w1_codes[:, t, :].bitcast(FP8X4),
+                    lhsT_scale=w1_plane[:, t, :],
                     rhs=words[:, inside : inside + BLOCK].bitcast(FP8X4),
                     rhs_scale=x_plane[:, first : first + BLOCK],
                     start=True,

@@ -26,19 +26,17 @@ def tile_picked_phpool_none_p_kernel(tc, x_words, x_scales, w1, w2, offs, out):
     with ExitStack() as ctx:
         keep = ctx.enter_context(tc.tile_pool(name="keep", bufs=1))
         ring = ctx.enter_context(tc.tile_pool(name="ring", bufs=4))
-        psum_a = ctx.enter_context(tc.psum_pool(name="psum_a", bufs=3))
-        psum_b = ctx.enter_context(tc.psum_pool(name="psum_b", bufs=3))
-        psum_o = ctx.enter_context(tc.psum_pool(name="psum_o", bufs=2))
+        psum = ctx.enter_context(tc.psum_pool(name="psum", bufs=1))
 
         offsets = keep.tile([P, S // 16], U16, name="offsets")
         nc.sync.dma_start(offsets[:], offs)
 
-        scale_table = keep.tile([P, T], U8, name="scale_table", align_bytes=64)
+        scale_table = keep.tile([P, T], U8, name="scale_table", tag="scales_then_w2", align_bytes=64)
         nc.vector.memset(scale_table[:].bitcast(I32), 0)
         x_plane = keep.tile([P, S], U8, name="x_plane", align_bytes=64)
         nc.vector.memset(x_plane[:].bitcast(I32), 0)
 
-        word_table = keep.tile([P, T], I32, name="word_table", align_bytes=64)
+        word_table = keep.tile([P, T], I32, name="word_table", tag="words_then_w2", align_bytes=64)
 
         w1_rows = w1.rearrange("(p j) c -> p j c", j=PACK)
         w1_raw = []
@@ -49,8 +47,6 @@ def tile_picked_phpool_none_p_kernel(tc, x_words, x_scales, w1, w2, offs, out):
             if n == 0:
                 nc.sync.dma_start(scale_table[0:P:8, :].bitcast(I32), x_scales[0].bitcast(I32))
         nc.sync.dma_start(word_table[:], x_words[0].rearrange("p n t -> p (n t)").bitcast(I32))
-        w2_raw = keep.tile([P, PACK, N], F32, name="w2_raw")
-        nc.sync.dma_start(w2_raw[:], w2.rearrange("(p j) n -> p j n", j=PACK))
 
         picked_scales = keep.tile([P, S], U8, name="picked_scales", align_bytes=64)
         nc.vector.tensor_copy(picked_scales[:], scale_table[:].indirect(offsets[:]))
@@ -58,10 +54,28 @@ def tile_picked_phpool_none_p_kernel(tc, x_words, x_scales, w1, w2, offs, out):
             nc.sync.dma_start(
                 x_plane[j:P:32, :].bitcast(I32), picked_scales[8 * j : P : 32, :].bitcast(I32)
             )
+        w2_raw = keep.tile([P, PACK, N], F32, name="w2_raw", tag="scales_then_w2", align_bytes=64)
+        nc.sync.dma_start(w2_raw[:], w2.rearrange("(p j) n -> p j n", j=PACK))
+
+        late_words = keep.tile([P, 2 * PIECE], I32, name="late_words", align_bytes=64)
+        nc.vector.memset(late_words[:], 0)
+        late_words = late_words[:].bitcast(U32)
+        warm_bank = psum.tile([P, 2 * PIECE], F32, name="warm_bank", tag="bank%d" % (S - BLOCK))
+        for width in (2 * PIECE, 2 * PIECE, BLOCK):
+            nc.tensor.matmul_mx(
+                out=warm_bank[:, :width],
+                lhsT=late_words[:, :P].bitcast(FP8X4),
+                lhsT_scale=picked_scales[:, :P],
+                rhs=late_words[:, :width].bitcast(FP8X4),
+                rhs_scale=picked_scales[:, :width],
+                start=True,
+                stop=True,
+            )
 
         w1_bf = keep.tile([P, PACK, P, PACK], BF16, name="w1_bf", align_bytes=64)
         for raw, (c0, c1) in zip(w1_raw, W1_CHUNKS):
-            nc.scalar.copy(
+            round_copy = nc.vector.tensor_copy if c1 == H else nc.scalar.copy
+            round_copy(
                 w1_bf[:, :, c0 // PACK : c1 // PACK, :].rearrange("p t m j -> p m t j"),
                 raw[:].rearrange("p j (m t) -> p m t j", t=PACK),
             )
@@ -77,16 +91,20 @@ def tile_picked_phpool_none_p_kernel(tc, x_words, x_scales, w1, w2, offs, out):
         for half in range(V // PIECE):
             for read in range(2):
                 first = read * V + half * PIECE
-                words = keep.tile([P, PIECE], U32, name="picked_words%d" % first, align_bytes=64)
+                if half == 0:
+                    tile = keep.tile([P, PIECE], U32, name="picked_words%d" % first, align_bytes=64)
+                    words = tile[:]
+                else:
+                    words = late_words[:, read * PIECE : (read + 1) * PIECE]
                 nc.vector.tensor_copy(
-                    words[:],
+                    words,
                     word_table[:].bitcast(U32).indirect(offsets[:, first // 16 : (first + PIECE) // 16]),
                 )
                 picked_words[first] = words
 
         w2_bf = keep.tile([P, N, PACK], BF16, name="w2_bf", align_bytes=64)
         nc.scalar.copy(w2_bf[:], w2_raw[:].rearrange("p j n -> p n j"))
-        w2_codes = keep.tile([P, N], U32, name="w2_codes", align_bytes=64)
+        w2_codes = keep.tile([P, N], U32, name="w2_codes", tag="words_then_w2", align_bytes=64)
         w2_plane = keep.tile([P, N], U8, name="w2_plane", align_bytes=64)
         nc.vector.quantize_mx(
             out=w2_codes[:].bitcast(FP8X4), scales=w2_plane[:], in_=w2_bf[:].rearrange("p n j -> p (n j)")
@@ -112,7 +130,7 @@ def tile_picked_phpool_none_p_kernel(tc, x_words, x_scales, w1, w2, offs, out):
             nc.vector.quantize_mx(
                 out=z_codes[:].bitcast(FP8X4), scales=z_plane[:], in_=z_bf[:].rearrange("p v t -> p (v t)")
             )
-            bank_o = psum_o.tile([P, BLOCK], F32, name="bank_o")
+            bank_o = psum.tile([P, BLOCK], F32, name="bank_o", tag="bank%d" % v0)
             nc.tensor.matmul_mx(
                 out=bank_o[:],
                 lhsT=w2_codes[:].bitcast(FP8X4),
@@ -126,17 +144,25 @@ def tile_picked_phpool_none_p_kernel(tc, x_words, x_scales, w1, w2, offs, out):
             nc.scalar.copy(result[:], bank_o[:])
             nc.sync.dma_start(out[:, v0 : v0 + BLOCK], result[:])
 
-        waiting = None
-        for v0 in range(0, V, BLOCK):
-            bank_a = psum_a.tile([P, PACK, BLOCK], F32, name="bank_a")
-            bank_b = psum_b.tile([P, PACK, BLOCK], F32, name="bank_b")
-            project(bank_a, v0)
-            project(bank_b, V + v0)
+        def first_layer(blocks):
+            for read in range(2):
+                for v0 in blocks:
+                    bank = psum.tile([P, PACK, BLOCK], F32, name="bank", tag="bank%d" % (read * V + v0))
+                    project(bank, read * V + v0)
+                    banks[read * V + v0] = bank
+
+        def larger_read(v0):
             first_read = ring.tile([P, BLOCK, PACK], F32, name="first_read")
-            nc.scalar.copy(first_read[:], bank_a[:].rearrange("p t v -> p v t"))
+            nc.scalar.copy(first_read[:], banks[v0][:].rearrange("p t v -> p v t"))
             z_bf = ring.tile([P, BLOCK, PACK], BF16, name="z_bf", align_bytes=64)
-            nc.vector.tensor_tensor(z_bf[:], bank_b[:].rearrange("p t v -> p v t"), first_read[:], MAX)
-            if waiting is not None:
-                second_layer(*waiting)
-            waiting = (v0, z_bf)
-        second_layer(*waiting)
+            nc.vector.tensor_tensor(z_bf[:], banks[V + v0][:].rearrange("p t v -> p v t"), first_read[:], MAX)
+            return z_bf
+
+        banks = {}
+        pairs = [range(v0, v0 + PIECE, BLOCK) for v0 in range(0, V, PIECE)]
+        for blocks in pairs:
+            first_layer(blocks)
+        for blocks in pairs:
+            pooled = [(v0, larger_read(v0)) for v0 in blocks]
+            for v0, z_bf in pooled:
+                second_layer(v0, z_bf)

@@ -18,7 +18,6 @@ P = 128
 PACK = 4
 PIECE = 256
 BLOCK = 128
-W1_CHUNKS = [(0, 128), (128, 384), (384, 512)]
 
 
 def tile_picked_phpool_none_p_kernel(tc, x_words, x_scales, w1, w2, offs, out):
@@ -39,13 +38,12 @@ def tile_picked_phpool_none_p_kernel(tc, x_words, x_scales, w1, w2, offs, out):
         word_table = keep.tile([P, T], I32, name="word_table", tag="words_then_w2", align_bytes=64)
 
         w1_rows = w1.rearrange("(p j) c -> p j c", j=PACK)
-        w1_raw = []
-        for n, (c0, c1) in enumerate(W1_CHUNKS):
-            raw = keep.tile([P, PACK, c1 - c0], F32, name="w1_raw%d" % n)
-            nc.sync.dma_start(raw[:], w1_rows[:, :, c0:c1])
-            w1_raw.append(raw)
-            if n == 0:
-                nc.sync.dma_start(scale_table[0:P:8, :].bitcast(I32), x_scales[0].bitcast(I32))
+        w1_low = keep.tile([P, 2, H], F32, name="w1_low")
+        w1_high = keep.tile([P, 2, H], F32, name="w1_high")
+        nc.sync.dma_start(w1_low[:, 0, :], w1_rows[:, 0, :])
+        nc.sync.dma_start(scale_table[0:P:8, :].bitcast(I32), x_scales[0].bitcast(I32))
+        nc.sync.dma_start(w1_low[:, 1, :], w1_rows[:, 1, :])
+        nc.sync.dma_start(w1_high[:], w1_rows[:, 2:4, :])
         nc.sync.dma_start(word_table[:], x_words[0].rearrange("p n t -> p (n t)").bitcast(I32))
 
         picked_scales = keep.tile([P, S], U8, name="picked_scales", align_bytes=64)
@@ -73,11 +71,14 @@ def tile_picked_phpool_none_p_kernel(tc, x_words, x_scales, w1, w2, offs, out):
             )
 
         w1_bf = keep.tile([P, PACK, P, PACK], BF16, name="w1_bf", align_bytes=64)
-        for raw, (c0, c1) in zip(w1_raw, W1_CHUNKS):
-            round_copy = nc.vector.tensor_copy if c1 == H else nc.scalar.copy
+        for raw, j0, m0, m1, round_copy in (
+            (w1_low, 0, 0, P, nc.scalar.copy),
+            (w1_high, 2, 0, P // 2, nc.scalar.copy),
+            (w1_high, 2, P // 2, P, nc.vector.tensor_copy),
+        ):
             round_copy(
-                w1_bf[:, :, c0 // PACK : c1 // PACK, :].rearrange("p t m j -> p m t j"),
-                raw[:].rearrange("p j (m t) -> p m t j", t=PACK),
+                w1_bf[:, :, m0:m1, j0 : j0 + 2].rearrange("p t m j -> p m t j"),
+                raw[:, :, m0 * PACK : m1 * PACK].rearrange("p j (m t) -> p m t j", t=PACK),
             )
         w1_codes = keep.tile([P, PACK, P], U32, name="w1_codes", align_bytes=64)
         w1_plane = keep.tile([P, PACK, P], U8, name="w1_plane", align_bytes=64)

@@ -35,6 +35,11 @@ def tile_picked_phpool_none_p_kernel(tc, x_words, x_scales, w1, w2, offs, out):
         x_plane = keep.tile([P, S], U8, name="x_plane", align_bytes=64)
         nc.vector.memset(x_plane[:].bitcast(I32), 0)
 
+        seed = keep.tile([P, 1], F32, name="seed")
+        nc.gpsimd.memset(seed[:], 0.0)
+        seed_bf = keep.tile([P, 1], BF16, name="seed_bf")
+        nc.scalar.copy(seed_bf[:], seed[:])
+
         word_table = keep.tile([P, T], I32, name="word_table", tag="words_then_w2", align_bytes=64)
 
         w1_rows = w1.rearrange("(p j) c -> p j c", j=PACK)

@@ -13,6 +13,8 @@ U16 = mybir.dt.uint16
 U8 = mybir.dt.uint8
 FP8X4 = mybir.dt.float8_e4m3fn_x4
 MAX = mybir.AluOpType.max
+MULT = mybir.AluOpType.mult
+ADD = mybir.AluOpType.add
 
 P = 128
 PACK = 4
@@ -64,13 +66,13 @@ def tile_picked_phpool_none_p_kernel(tc, x_words, x_scales, w1, w2, offs, out):
         nc.vector.memset(late_words[:], 0)
         late_words = late_words[:].bitcast(U32)
         warm_bank = psum.tile([P, 2 * PIECE], F32, name="warm_bank", tag="bank%d" % (S - BLOCK))
-        for width in (2 * PIECE, 2 * PIECE, BLOCK):
+        for warm in range(3):
             nc.tensor.matmul_mx(
-                out=warm_bank[:, :width],
-                lhsT=late_words[:, :P].bitcast(FP8X4),
-                lhsT_scale=picked_scales[:, :P],
-                rhs=late_words[:, :width].bitcast(FP8X4),
-                rhs_scale=picked_scales[:, :width],
+                out=warm_bank[: P // 2, :],
+                lhsT=late_words[:, : P // 2].bitcast(FP8X4),
+                lhsT_scale=picked_scales[:, : P // 2],
+                rhs=late_words.bitcast(FP8X4),
+                rhs_scale=picked_scales[:, : 2 * PIECE],
                 start=True,
                 stop=True,
             )
@@ -108,13 +110,8 @@ def tile_picked_phpool_none_p_kernel(tc, x_words, x_scales, w1, w2, offs, out):
                 )
                 picked_words[first] = words
 
-        w2_bf = keep.tile([P, N, PACK], BF16, name="w2_bf", align_bytes=64)
-        nc.scalar.copy(w2_bf[:], w2_raw[:].rearrange("p j n -> p n j"))
-        w2_codes = keep.tile([P, N], U32, name="w2_codes", tag="words_then_w2", align_bytes=64)
-        w2_plane = keep.tile([P, N], U8, name="w2_plane", align_bytes=64)
-        nc.vector.quantize_mx(
-            out=w2_codes[:].bitcast(FP8X4), scales=w2_plane[:], in_=w2_bf[:].rearrange("p n j -> p (n j)")
-        )
+        w2_and_z = keep.tile([P, N + BLOCK, PACK], BF16, name="w2_and_z", tag="words_then_w2", align_bytes=64)
+        nc.gpsimd.tensor_scalar(w2_and_z[:, :N, :], w2_raw[:].rearrange("p j n -> p n j"), 1.0, 0.0, MULT, ADD)
 
         def project(bank, first):
             words = picked_words[first // PIECE * PIECE]
@@ -130,45 +127,58 @@ def tile_picked_phpool_none_p_kernel(tc, x_words, x_scales, w1, w2, offs, out):
                     stop=True,
                 )
 
-        def second_layer(v0, z_bf):
-            z_codes = ring.tile([P, BLOCK], U32, name="z_codes", align_bytes=64)
-            z_plane = ring.tile([P, BLOCK], U8, name="z_plane", align_bytes=64)
+        def quantise(values):
+            width = values.shape[1]
+            codes = ring.tile([P, width], U32, name="codes", align_bytes=64)
+            plane = ring.tile([P, width], U8, name="plane", align_bytes=64)
             nc.vector.quantize_mx(
-                out=z_codes[:].bitcast(FP8X4), scales=z_plane[:], in_=z_bf[:].rearrange("p v t -> p (v t)")
+                out=codes[:].bitcast(FP8X4), scales=plane[:], in_=values.rearrange("p v t -> p (v t)")
             )
+            return codes[:], plane[:]
+
+        def second_layer(v0, z_codes, z_plane, copy_out):
             bank_o = psum.tile([P, BLOCK], F32, name="bank_o", tag="bank%d" % v0)
             nc.tensor.matmul_mx(
                 out=bank_o[:],
-                lhsT=w2_codes[:].bitcast(FP8X4),
-                lhsT_scale=w2_plane[:],
-                rhs=z_codes[:].bitcast(FP8X4),
-                rhs_scale=z_plane[:],
+                lhsT=w2_codes.bitcast(FP8X4),
+                lhsT_scale=w2_plane,
+                rhs=z_codes.bitcast(FP8X4),
+                rhs_scale=z_plane,
                 start=True,
                 stop=True,
             )
             result = ring.tile([P, BLOCK], F32, name="result")
-            nc.scalar.copy(result[:], bank_o[:])
+            copy_out(result[:], bank_o[:])
             nc.sync.dma_start(out[:, v0 : v0 + BLOCK], result[:])
 
-        def first_layer(blocks):
+        banks = {}
+        for first_block in range(0, V, PIECE):
             for read in range(2):
-                for v0 in blocks:
+                for v0 in range(first_block, first_block + PIECE, BLOCK):
                     bank = psum.tile([P, PACK, BLOCK], F32, name="bank", tag="bank%d" % (read * V + v0))
                     project(bank, read * V + v0)
-                    banks[read * V + v0] = bank
+                    banks[read * V + v0] = bank[:].rearrange("p t v -> p v t")
 
-        def larger_read(v0):
+        last = V - BLOCK
+        staged = {}
+        for v0 in range(0, last, BLOCK):
             first_read = ring.tile([P, BLOCK, PACK], F32, name="first_read")
-            nc.scalar.copy(first_read[:], banks[v0][:].rearrange("p t v -> p v t"))
-            z_bf = ring.tile([P, BLOCK, PACK], BF16, name="z_bf", align_bytes=64)
-            nc.vector.tensor_tensor(z_bf[:], banks[V + v0][:].rearrange("p t v -> p v t"), first_read[:], MAX)
-            return z_bf
+            nc.scalar.copy(first_read[:], banks[v0])
+            staged[v0] = first_read
+        last_reads = keep.tile([P, 2, BLOCK, PACK], BF16, name="last_reads", align_bytes=64)
+        for read in range(2):
+            nc.scalar.copy(last_reads[:, read], banks[read * V + last])
 
-        banks = {}
-        pairs = [range(v0, v0 + PIECE, BLOCK) for v0 in range(0, V, PIECE)]
-        for blocks in pairs:
-            first_layer(blocks)
-        for blocks in pairs:
-            pooled = [(v0, larger_read(v0)) for v0 in blocks]
-            for v0, z_bf in pooled:
-                second_layer(v0, z_bf)
+        z_rest = keep.tile([P, 3, BLOCK, PACK], BF16, name="z_rest", align_bytes=64)
+        z_of = {0: z_rest[:, 0], BLOCK: w2_and_z[:, N:, :], PIECE: z_rest[:, 1], last: z_rest[:, 2]}
+        for v0 in range(0, PIECE, BLOCK):
+            nc.vector.tensor_tensor(z_of[v0], banks[V + v0], staged[v0][:], MAX)
+        first_z = quantise(z_of[0])
+        both_codes, both_plane = quantise(w2_and_z[:])
+        w2_codes, w2_plane = both_codes[:, :N], both_plane[:, :N]
+        second_layer(0, *first_z, nc.scalar.copy)
+        second_layer(BLOCK, both_codes[:, N:], both_plane[:, N:], nc.scalar.copy)
+        nc.vector.tensor_tensor(z_of[PIECE], banks[V + PIECE], staged[PIECE][:], MAX)
+        nc.vector.tensor_tensor(z_of[last], last_reads[:, 0], last_reads[:, 1], MAX)
+        for v0 in range(PIECE, V, BLOCK):
+            second_layer(v0, *quantise(z_of[v0]), nc.vector.tensor_copy if v0 == last else nc.scalar.copy)

@@ -29,6 +29,10 @@ def tile_picked_phpool_none_p_kernel(tc, x_words, x_scales, w1, w2, offs, out):
         ring = ctx.enter_context(tc.tile_pool(name="ring", bufs=4))
         psum = ctx.enter_context(tc.psum_pool(name="psum", bufs=1))
 
+        w1_rows = w1.rearrange("(p j) c -> p j c", j=PACK)
+        w1_raw = keep.tile([P, PACK, H], F32, name="w1_raw")
+        nc.sync.dma_start(w1_raw[:, 0, :], w1_rows[:, 0, :])
+
         offsets = keep.tile([P, S // 16], U16, name="offsets")
         nc.sync.dma_start(offsets[:], offs)
 
@@ -44,13 +48,8 @@ def tile_picked_phpool_none_p_kernel(tc, x_words, x_scales, w1, w2, offs, out):
 
         word_table = keep.tile([P, T], I32, name="word_table", tag="words_then_w2", align_bytes=64)
 
-        w1_rows = w1.rearrange("(p j) c -> p j c", j=PACK)
-        w1_low = keep.tile([P, 2, H], F32, name="w1_low")
-        w1_high = keep.tile([P, 2, H], F32, name="w1_high")
-        nc.sync.dma_start(w1_low[:, 0, :], w1_rows[:, 0, :])
         nc.sync.dma_start(scale_table[0:P:8, :].bitcast(I32), x_scales[0].bitcast(I32))
-        nc.sync.dma_start(w1_low[:, 1, :], w1_rows[:, 1, :])
-        nc.sync.dma_start(w1_high[:], w1_rows[:, 2:4, :])
+        nc.sync.dma_start(w1_raw[:, 1:PACK, :], w1_rows[:, 1:PACK, :])
         nc.sync.dma_start(word_table[:], x_words[0].rearrange("p n t -> p (n t)").bitcast(I32))
 
         picked_scales = keep.tile([P, S], U8, name="picked_scales", align_bytes=64)
@@ -78,14 +77,10 @@ def tile_picked_phpool_none_p_kernel(tc, x_words, x_scales, w1, w2, offs, out):
             )
 
         w1_bf = keep.tile([P, PACK, P, PACK], BF16, name="w1_bf", align_bytes=64)
-        for raw, j0, m0, m1, round_copy in (
-            (w1_low, 0, 0, P, nc.scalar.copy),
-            (w1_high, 2, 0, P // 2, nc.scalar.copy),
-            (w1_high, 2, P // 2, P, nc.vector.tensor_copy),
-        ):
+        for m0, m1, round_copy in ((0, P // 2, nc.scalar.copy), (P // 2, P, nc.vector.tensor_copy)):
             round_copy(
-                w1_bf[:, :, m0:m1, j0 : j0 + 2].rearrange("p t m j -> p m t j"),
-                raw[:, :, m0 * PACK : m1 * PACK].rearrange("p j (m t) -> p m t j", t=PACK),
+                w1_bf[:, :, m0:m1, :].rearrange("p t m j -> p m t j"),
+                w1_raw[:, :, m0 * PACK : m1 * PACK].rearrange("p j (m t) -> p m t j", t=PACK),
             )
         w1_codes = keep.tile([P, PACK, P], U32, name="w1_codes", align_bytes=64)
         w1_plane = keep.tile([P, PACK, P], U8, name="w1_plane", align_bytes=64)

@@ -42,7 +42,7 @@ def tile_picked_phpool_none_p_kernel(tc, x_words, x_scales, w1, w2, offs, out):
         nc.vector.memset(x_plane[:].bitcast(I32), 0)
 
         seed = keep.tile([P, 1], F32, name="seed")
-        nc.gpsimd.memset(seed[:], 0.0)
+        nc.vector.memset(seed[:], 0.0)
         seed_bf = keep.tile([P, 1], BF16, name="seed_bf")
         nc.scalar.copy(seed_bf[:], seed[:])
 

@@ -59,7 +59,9 @@ def tile_picked_phpool_none_p_kernel(tc, x_words, x_scales, w1, w2, offs, out):
                 x_plane[j:P:32, :].bitcast(I32), picked_scales[8 * j : P : 32, :].bitcast(I32)
             )
         w2_raw = keep.tile([P, PACK, N], F32, name="w2_raw", tag="scales_then_w2", align_bytes=64)
-        nc.sync.dma_start(w2_raw[:], w2.rearrange("(p j) n -> p j n", j=PACK))
+        w2_rows = w2.rearrange("(a t r) n -> r a t n", t=PACK, r=2)
+        for r in range(2):
+            nc.sync.dma_start(w2_raw[r:P:2], w2_rows[r])
 
         late_words = keep.tile([P, 2 * PIECE], I32, name="late_words", align_bytes=64)
         nc.vector.memset(late_words[:], 0)
@@ -77,18 +79,19 @@ def tile_picked_phpool_none_p_kernel(tc, x_words, x_scales, w1, w2, offs, out):
             )
 
         w1_bf = keep.tile([P, PACK, P, PACK], BF16, name="w1_bf", align_bytes=64)
-        for m0, m1, round_copy in ((0, P // 2, nc.scalar.copy), (P // 2, P, nc.vector.tensor_copy)):
+        for u, round_copy in ((0, nc.scalar.copy), (1, nc.vector.tensor_copy)):
             round_copy(
-                w1_bf[:, :, m0:m1, :].rearrange("p t m j -> p m t j"),
-                w1_raw[:, :, m0 * PACK : m1 * PACK].rearrange("p j (m t) -> p m t j", t=PACK),
+                w1_bf[:, 2 * u : 2 * u + 2].rearrange("p t (a r) j -> p a t r j", r=2),
+                w1_raw[:].rearrange("p j (a u t r) -> p u a t r j", u=2, t=2, r=2)[:, u],
             )
         w1_codes = keep.tile([P, PACK, P], U32, name="w1_codes", align_bytes=64)
         w1_plane = keep.tile([P, PACK, P], U8, name="w1_plane", align_bytes=64)
-        nc.vector.quantize_mx(
-            out=w1_codes[:].rearrange("p t m -> p (t m)").bitcast(FP8X4),
-            scales=w1_plane[:].rearrange("p t m -> p (t m)"),
-            in_=w1_bf[:].rearrange("p t m j -> p (t m j)"),
-        )
+        for t0 in (0, 2):
+            nc.vector.quantize_mx(
+                out=w1_codes[:, t0 : t0 + 2].rearrange("p t m -> p (t m)").bitcast(FP8X4),
+                scales=w1_plane[:, t0 : t0 + 2].rearrange("p t m -> p (t m)"),
+                in_=w1_bf[:, t0 : t0 + 2].rearrange("p t m j -> p (t m j)"),
+            )
 
         picked_words = {}
         for half in range(V // PIECE):

@@ -63,20 +63,7 @@ def tile_picked_phpool_none_p_kernel(tc, x_words, x_scales, w1, w2, offs, out):
         for r in range(2):
             nc.sync.dma_start(w2_raw[r:P:2], w2_rows[r])
 
-        late_words = keep.tile([P, 2 * PIECE], I32, name="late_words", align_bytes=64)
-        nc.vector.memset(late_words[:], 0)
-        late_words = late_words[:].bitcast(U32)
-        warm_bank = psum.tile([P, 2 * PIECE], F32, name="warm_bank", tag="bank%d" % (S - BLOCK))
-        for warm in range(3):
-            nc.tensor.matmul_mx(
-                out=warm_bank[: P // 2, :],
-                lhsT=late_words[:, : P // 2].bitcast(FP8X4),
-                lhsT_scale=picked_scales[:, : P // 2],
-                rhs=late_words.bitcast(FP8X4),
-                rhs_scale=picked_scales[:, : 2 * PIECE],
-                start=True,
-                stop=True,
-            )
+        late_words = keep.tile([P, 2 * PIECE], U32, name="late_words", align_bytes=64)
 
         w1_bf = keep.tile([P, PACK, P, PACK], BF16, name="w1_bf", align_bytes=64)
         for u, round_copy in ((0, nc.scalar.copy), (1, nc.vector.tensor_copy)):

@@ -80,6 +80,20 @@ def tile_picked_phpool_none_p_kernel(tc, x_words, x_scales, w1, w2, offs, out):
                 in_=w1_bf[:, t0 : t0 + 2].rearrange("p t m j -> p (t m j)"),
             )
 
+        all_codes = w1_codes[:].rearrange("p t m -> p (t m)").bitcast(FP8X4)
+        all_planes = w1_plane[:].rearrange("p t m -> p (t m)")
+        warm_bank = psum.tile([P, H], F32, name="warm_bank", tag="bank%d" % (S - BLOCK))
+        for width in (BLOCK, BLOCK, H, H):
+            nc.tensor.matmul_mx(
+                out=warm_bank[:32, :width],
+                lhsT=all_codes[:, H // 2 : H // 2 + 32],
+                lhsT_scale=all_planes[:, H // 2 : H // 2 + 32],
+                rhs=all_codes[:, H - width :],
+                rhs_scale=all_planes[:, H - width :],
+                start=True,
+                stop=True,
+            )
+
         picked_words = {}
         for half in range(V // PIECE):
             for read in range(2):

@@ -66,14 +66,18 @@ def tile_picked_phpool_none_p_kernel(tc, x_words, x_scales, w1, w2, offs, out):
         late_words = keep.tile([P, 2 * PIECE], U32, name="late_words", align_bytes=64)
 
         w1_bf = keep.tile([P, PACK, P, PACK], BF16, name="w1_bf", align_bytes=64)
-        for u, round_copy in ((0, nc.scalar.copy), (1, nc.vector.tensor_copy)):
+        for u, a0, a1, round_copy in (
+            (0, 0, 52, nc.scalar.copy),
+            (1, 0, 64, nc.vector.tensor_copy),
+            (0, 52, 64, nc.vector.tensor_copy),
+        ):
             round_copy(
-                w1_bf[:, 2 * u : 2 * u + 2].rearrange("p t (a r) j -> p a t r j", r=2),
-                w1_raw[:].rearrange("p j (a u t r) -> p u a t r j", u=2, t=2, r=2)[:, u],
+                w1_bf[:, 2 * u : 2 * u + 2].rearrange("p t (a r) j -> p a j t r", r=2)[:, a0:a1],
+                w1_raw[:].rearrange("p j (a u t r) -> p u a j t r", u=2, t=2, r=2)[:, u, a0:a1],
             )
         w1_codes = keep.tile([P, PACK, P], U32, name="w1_codes", align_bytes=64)
         w1_plane = keep.tile([P, PACK, P], U8, name="w1_plane", align_bytes=64)
-        for t0 in (0, 2):
+        for t0 in (2, 0):
             nc.vector.quantize_mx(
                 out=w1_codes[:, t0 : t0 + 2].rearrange("p t m -> p (t m)").bitcast(FP8X4),
                 scales=w1_plane[:, t0 : t0 + 2].rearrange("p t m -> p (t m)"),
@@ -126,9 +130,9 @@ def tile_picked_phpool_none_p_kernel(tc, x_words, x_scales, w1, w2, offs, out):
                     stop=True,
                 )
 
-        def quantise(values):
+        def quantise(values, tag):
             width = values.shape[1]
-            codes = ring.tile([P, width], U32, name="codes", align_bytes=64)
+            codes = keep.tile([P, width], U32, name="codes", tag=tag, align_bytes=64)
             plane = ring.tile([P, width], U8, name="plane", align_bytes=64)
             nc.vector.quantize_mx(
                 out=codes[:].bitcast(FP8X4), scales=plane[:], in_=values.rearrange("p v t -> p (v t)")
@@ -151,12 +155,15 @@ def tile_picked_phpool_none_p_kernel(tc, x_words, x_scales, w1, w2, offs, out):
             nc.sync.dma_start(out[:, v0 : v0 + BLOCK], result[:])
 
         banks = {}
-        for first_block in range(0, V, PIECE):
-            for read in range(2):
-                for v0 in range(first_block, first_block + PIECE, BLOCK):
-                    bank = psum.tile([P, PACK, BLOCK], F32, name="bank", tag="bank%d" % (read * V + v0))
-                    project(bank, read * V + v0)
-                    banks[read * V + v0] = bank[:].rearrange("p t v -> p v t")
+        order = [0]
+        for v0 in range(0, V, BLOCK):
+            if v0 + BLOCK < V:
+                order.append(v0 + BLOCK)
+            order.append(V + v0)
+        for first in order:
+            bank = psum.tile([P, PACK, BLOCK], F32, name="bank", tag="bank%d" % first)
+            project(bank, first)
+            banks[first] = bank[:].rearrange("p t v -> p v t")
 
         last = V - BLOCK
         staged = {}
@@ -172,12 +179,12 @@ def tile_picked_phpool_none_p_kernel(tc, x_words, x_scales, w1, w2, offs, out):
         z_of = {0: z_rest[:, 0], BLOCK: w2_and_z[:, N:, :], PIECE: z_rest[:, 1], last: z_rest[:, 2]}
         for v0 in range(0, PIECE, BLOCK):
             nc.vector.tensor_tensor(z_of[v0], banks[V + v0], staged[v0][:], MAX)
-        first_z = quantise(z_of[0])
-        both_codes, both_plane = quantise(w2_and_z[:])
+        first_z = quantise(z_of[0], "codes_first")
+        both_codes, both_plane = quantise(w2_and_z[:], "codes_both")
         w2_codes, w2_plane = both_codes[:, :N], both_plane[:, :N]
         second_layer(0, *first_z, nc.scalar.copy)
         second_layer(BLOCK, both_codes[:, N:], both_plane[:, N:], nc.scalar.copy)
         nc.vector.tensor_tensor(z_of[PIECE], banks[V + PIECE], staged[PIECE][:], MAX)
         nc.vector.tensor_tensor(z_of[last], last_reads[:, 0], last_reads[:, 1], MAX)
         for v0 in range(PIECE, V, BLOCK):
-            second_layer(v0, *quantise(z_of[v0]), nc.vector.tensor_copy if v0 == last else nc.scalar.copy)
+            second_layer(v0, *quantise(z_of[v0], "codes%d" % v0), nc.vector.tensor_copy if v0 == last else nc.scalar.copy)

@@ -87,7 +87,7 @@ def tile_picked_phpool_none_p_kernel(tc, x_words, x_scales, w1, w2, offs, out):
         all_codes = w1_codes[:].rearrange("p t m -> p (t m)").bitcast(FP8X4)
         all_planes = w1_plane[:].rearrange("p t m -> p (t m)")
         warm_bank = psum.tile([P, H], F32, name="warm_bank", tag="bank%d" % (S - BLOCK))
-        for width in (BLOCK, BLOCK, H, H):
+        for width in (BLOCK, BLOCK, BLOCK, H, BLOCK):
             nc.tensor.matmul_mx(
                 out=warm_bank[:32, :width],
                 lhsT=all_codes[:, H // 2 : H // 2 + 32],

@@ -20,6 +20,7 @@ P = 128
 PACK = 4
 PIECE = 256
 BLOCK = 128
+HALF = 64
 
 
 def tile_picked_phpool_none_p_kernel(tc, x_words, x_scales, w1, w2, offs, out):
@@ -63,8 +64,6 @@ def tile_picked_phpool_none_p_kernel(tc, x_words, x_scales, w1, w2, offs, out):
         for r in range(2):
             nc.sync.dma_start(w2_raw[r:P:2], w2_rows[r])
 
-        late_words = keep.tile([P, 2 * PIECE], U32, name="late_words", align_bytes=64)
-
         w1_bf = keep.tile([P, PACK, P, PACK], BF16, name="w1_bf", align_bytes=64)
         for u, a0, a1, round_copy in (
             (0, 0, 52, nc.scalar.copy),
@@ -102,11 +101,7 @@ def tile_picked_phpool_none_p_kernel(tc, x_words, x_scales, w1, w2, offs, out):
         for half in range(V // PIECE):
             for read in range(2):
                 first = read * V + half * PIECE
-                if half == 0:
-                    tile = keep.tile([P, PIECE], U32, name="picked_words%d" % first, align_bytes=64)
-                    words = tile[:]
-                else:
-                    words = late_words[:, read * PIECE : (read + 1) * PIECE]
+                words = keep.tile([P, PIECE], U32, name="words", tag="words%d" % first, align_bytes=64)[:]
                 nc.vector.tensor_copy(
                     words,
                     word_table[:].bitcast(U32).indirect(offsets[:, first // 16 : (first + PIECE) // 16]),
@@ -133,26 +128,30 @@ def tile_picked_phpool_none_p_kernel(tc, x_words, x_scales, w1, w2, offs, out):
         def quantise(values, tag):
             width = values.shape[1]
             codes = keep.tile([P, width], U32, name="codes", tag=tag, align_bytes=64)
-            plane = ring.tile([P, width], U8, name="plane", align_bytes=64)
+            plane = keep.tile([P, width], U8, name="plane", tag=tag + "_plane", align_bytes=64)
             nc.vector.quantize_mx(
                 out=codes[:].bitcast(FP8X4), scales=plane[:], in_=values.rearrange("p v t -> p (v t)")
             )
             return codes[:], plane[:]
 
-        def second_layer(v0, z_codes, z_plane, copy_out):
-            bank_o = psum.tile([P, BLOCK], F32, name="bank_o", tag="bank%d" % v0)
-            nc.tensor.matmul_mx(
-                out=bank_o[:],
-                lhsT=w2_codes.bitcast(FP8X4),
-                lhsT_scale=w2_plane,
-                rhs=z_codes.bitcast(FP8X4),
-                rhs_scale=z_plane,
-                start=True,
-                stop=True,
-            )
-            result = ring.tile([P, BLOCK], F32, name="result")
+        def second_layer(v0, parts, copy_out):
+            width = sum(z_codes.shape[1] for z_codes, z_plane in parts)
+            bank_o = psum.tile([P, width], F32, name="bank_o", tag="bank%d" % (v0 if v0 % BLOCK == 0 else V))
+            column = 0
+            for z_codes, z_plane in parts:
+                nc.tensor.matmul_mx(
+                    out=bank_o[:, column : column + z_codes.shape[1]],
+                    lhsT=w2_codes.bitcast(FP8X4),
+                    lhsT_scale=w2_plane,
+                    rhs=z_codes.bitcast(FP8X4),
+                    rhs_scale=z_plane,
+                    start=True,
+                    stop=True,
+                )
+                column = column + z_codes.shape[1]
+            result = keep.tile([P, width], F32, name="result", tag="result%d" % v0)
             copy_out(result[:], bank_o[:])
-            nc.sync.dma_start(out[:, v0 : v0 + BLOCK], result[:])
+            nc.sync.dma_start(out[:, v0 : v0 + width], result[:])
 
         banks = {}
         order = [0]
@@ -172,19 +171,22 @@ def tile_picked_phpool_none_p_kernel(tc, x_words, x_scales, w1, w2, offs, out):
             nc.scalar.copy(first_read[:], banks[v0])
             staged[v0] = first_read
         last_reads = keep.tile([P, 2, BLOCK, PACK], BF16, name="last_reads", align_bytes=64)
-        for read in range(2):
-            nc.scalar.copy(last_reads[:, read], banks[read * V + last])
+        nc.scalar.copy(last_reads[:, 0], banks[last])
+        for h in range(0, BLOCK, HALF):
+            nc.scalar.copy(last_reads[:, 1, h : h + HALF], banks[V + last][:, h : h + HALF])
 
         z_rest = keep.tile([P, 3, BLOCK, PACK], BF16, name="z_rest", align_bytes=64)
         z_of = {0: z_rest[:, 0], BLOCK: w2_and_z[:, N:, :], PIECE: z_rest[:, 1], last: z_rest[:, 2]}
         for v0 in range(0, PIECE, BLOCK):
             nc.vector.tensor_tensor(z_of[v0], banks[V + v0], staged[v0][:], MAX)
-        first_z = quantise(z_of[0], "codes_first")
-        both_codes, both_plane = quantise(w2_and_z[:], "codes_both")
-        w2_codes, w2_plane = both_codes[:, :N], both_plane[:, :N]
-        second_layer(0, *first_z, nc.scalar.copy)
-        second_layer(BLOCK, both_codes[:, N:], both_plane[:, N:], nc.scalar.copy)
+        first_z = quantise(z_of[0], "words%d" % PIECE)
         nc.vector.tensor_tensor(z_of[PIECE], banks[V + PIECE], staged[PIECE][:], MAX)
-        nc.vector.tensor_tensor(z_of[last], last_reads[:, 0], last_reads[:, 1], MAX)
-        for v0 in range(PIECE, V, BLOCK):
-            second_layer(v0, *quantise(z_of[v0], "codes%d" % v0), nc.vector.tensor_copy if v0 == last else nc.scalar.copy)
+        both_codes, both_plane = quantise(w2_and_z[:], "words%d" % (V + PIECE))
+        w2_codes, w2_plane = both_codes[:, :N], both_plane[:, :N]
+        second_layer(0, [first_z, (both_codes[:, N:], both_plane[:, N:])], nc.scalar.copy)
+        early, late = slice(0, HALF), slice(HALF, BLOCK)
+        nc.vector.tensor_tensor(z_of[last][:, early], last_reads[:, 0, early], last_reads[:, 1, early], MAX)
+        second_layer(PIECE, [quantise(z_of[PIECE], "codes_third")], nc.scalar.copy)
+        nc.vector.tensor_tensor(z_of[last][:, late], last_reads[:, 0, late], last_reads[:, 1, late], MAX)
+        second_layer(last, [quantise(z_of[last][:, early], "codes_early")], nc.scalar.copy)
+        second_layer(last + HALF, [quantise(z_of[last][:, late], "codes_late")], nc.vector.tensor_copy)

@@ -21,6 +21,7 @@ PACK = 4
 PIECE = 256
 BLOCK = 128
 HALF = 64
+RUN = 4
 
 
 def tile_picked_phpool_none_p_kernel(tc, x_words, x_scales, w1, w2, offs, out):
@@ -60,39 +61,48 @@ def tile_picked_phpool_none_p_kernel(tc, x_words, x_scales, w1, w2, offs, out):
                 x_plane[j:P:32, :].bitcast(I32), picked_scales[8 * j : P : 32, :].bitcast(I32)
             )
         w2_raw = keep.tile([P, PACK, N], F32, name="w2_raw", tag="scales_then_w2", align_bytes=64)
-        w2_rows = w2.rearrange("(a t r) n -> r a t n", t=PACK, r=2)
-        for r in range(2):
-            nc.sync.dma_start(w2_raw[r:P:2], w2_rows[r])
+        w2_rows = w2.rearrange("(a t r) n -> r a t n", t=PACK, r=RUN)
+        for r in range(RUN):
+            nc.sync.dma_start(w2_raw[r:P:RUN], w2_rows[r])
 
-        w1_bf = keep.tile([P, PACK, P, PACK], BF16, name="w1_bf", align_bytes=64)
-        for u, a0, a1, round_copy in (
-            (0, 0, 52, nc.scalar.copy),
-            (1, 0, 64, nc.vector.tensor_copy),
-            (0, 52, 64, nc.vector.tensor_copy),
-        ):
-            round_copy(
-                w1_bf[:, 2 * u : 2 * u + 2].rearrange("p t (a r) j -> p a j t r", r=2)[:, a0:a1],
-                w1_raw[:].rearrange("p j (a u t r) -> p u a j t r", u=2, t=2, r=2)[:, u, a0:a1],
-            )
+        w1_by_tile = w1_raw[:].rearrange("p j (a t r) -> p t a j r", t=PACK, r=RUN)
         w1_codes = keep.tile([P, PACK, P], U32, name="w1_codes", align_bytes=64)
         w1_plane = keep.tile([P, PACK, P], U8, name="w1_plane", align_bytes=64)
-        for t0 in (2, 0):
-            nc.vector.quantize_mx(
-                out=w1_codes[:, t0 : t0 + 2].rearrange("p t m -> p (t m)").bitcast(FP8X4),
-                scales=w1_plane[:, t0 : t0 + 2].rearrange("p t m -> p (t m)"),
-                in_=w1_bf[:, t0 : t0 + 2].rearrange("p t m j -> p (t m j)"),
+
+        rounded = [keep.tile([P, P, PACK], BF16, name="w1_bf", tag="w1_bf%d" % t, align_bytes=64) for t in range(PACK)]
+
+        def round_w1(round_copy, t, rows):
+            round_copy(
+                rounded[t][:].rearrange("p (a r) j -> p a j r", r=RUN)[:, :, rows], w1_by_tile[:, t, :, rows]
             )
+
+        def quantise_w1(t):
+            nc.vector.quantize_mx(
+                out=w1_codes[:, t].bitcast(FP8X4),
+                scales=w1_plane[:, t],
+                in_=rounded[t][:].rearrange("p m j -> p (m j)"),
+            )
+
+        late_rows = slice(1, PACK)
+        for t in range(2):
+            round_w1(nc.scalar.copy, t, slice(0, 1))
+        for t in range(2):
+            round_w1(nc.scalar.copy, t, late_rows)
+        for t in range(2, PACK):
+            round_w1(nc.vector.tensor_copy, t, slice(0, PACK))
+        for t in (2, 3, 0, 1):
+            quantise_w1(t)
 
         all_codes = w1_codes[:].rearrange("p t m -> p (t m)").bitcast(FP8X4)
         all_planes = w1_plane[:].rearrange("p t m -> p (t m)")
         warm_bank = psum.tile([P, H], F32, name="warm_bank", tag="bank%d" % (S - BLOCK))
-        for width in (BLOCK, BLOCK, BLOCK, H, BLOCK):
+        for first, width in ((2 * P, P), (2 * P, P), (2 * P, P), (2 * P, P), (0, H)):
             nc.tensor.matmul_mx(
                 out=warm_bank[:32, :width],
-                lhsT=all_codes[:, H // 2 : H // 2 + 32],
-                lhsT_scale=all_planes[:, H // 2 : H // 2 + 32],
-                rhs=all_codes[:, H - width :],
-                rhs_scale=all_planes[:, H - width :],
+                lhsT=all_codes[:, 2 * P : 2 * P + 32],
+                lhsT_scale=all_planes[:, 2 * P : 2 * P + 32],
+                rhs=all_codes[:, first : first + width],
+                rhs_scale=all_planes[:, first : first + width],
                 start=True,
                 stop=True,
             )
@@ -188,5 +198,5 @@ def tile_picked_phpool_none_p_kernel(tc, x_words, x_scales, w1, w2, offs, out):
         nc.vector.tensor_tensor(z_of[last][:, early], last_reads[:, 0, early], last_reads[:, 1, early], MAX)
         second_layer(PIECE, [quantise(z_of[PIECE], "codes_third")], nc.scalar.copy)
         nc.vector.tensor_tensor(z_of[last][:, late], last_reads[:, 0, late], last_reads[:, 1, late], MAX)
-        second_layer(last, [quantise(z_of[last][:, early], "codes_early")], nc.scalar.copy)
-        second_layer(last + HALF, [quantise(z_of[last][:, late], "codes_late")], nc.vector.tensor_copy)
+        halves = [quantise(z_of[last][:, early], "codes_early"), quantise(z_of[last][:, late], "codes_late")]
+        second_layer(last, halves, nc.vector.tensor_copy)

@@ -190,10 +190,10 @@ def tile_picked_phpool_none_p_kernel(tc, x_words, x_scales, w1, w2, offs, out):
         for v0 in range(0, PIECE, BLOCK):
             nc.vector.tensor_tensor(z_of[v0], banks[V + v0], staged[v0][:], MAX)
         first_z = quantise(z_of[0], "words%d" % PIECE)
-        nc.vector.tensor_tensor(z_of[PIECE], banks[V + PIECE], staged[PIECE][:], MAX)
-        both_codes, both_plane = quantise(w2_and_z[:], "words%d" % (V + PIECE))
+        both_codes, both_plane = quantise(w2_and_z[:], "codes_both")
         w2_codes, w2_plane = both_codes[:, :N], both_plane[:, :N]
         second_layer(0, [first_z, (both_codes[:, N:], both_plane[:, N:])], nc.scalar.copy)
+        nc.vector.tensor_tensor(z_of[PIECE], banks[V + PIECE], staged[PIECE][:], MAX)
         early, late = slice(0, HALF), slice(HALF, BLOCK)
         nc.vector.tensor_tensor(z_of[last][:, early], last_reads[:, 0, early], last_reads[:, 1, early], MAX)
         second_layer(PIECE, [quantise(z_of[PIECE], "codes_third")], nc.scalar.copy)

@@ -43,11 +43,6 @@ def tile_picked_phpool_none_p_kernel(tc, x_words, x_scales, w1, w2, offs, out):
         x_plane = keep.tile([P, S], U8, name="x_plane", align_bytes=64)
         nc.vector.memset(x_plane[:].bitcast(I32), 0)
 
-        seed = keep.tile([P, 1], F32, name="seed")
-        nc.vector.memset(seed[:], 0.0)
-        seed_bf = keep.tile([P, 1], BF16, name="seed_bf")
-        nc.scalar.copy(seed_bf[:], seed[:])
-
         word_table = keep.tile([P, T], I32, name="word_table", tag="words_then_w2", align_bytes=64)
 
         nc.sync.dma_start(scale_table[0:P:8, :].bitcast(I32), x_scales[0].bitcast(I32))

from contextlib import ExitStack

import concourse.mybir as mybir

K, T, S, H, N, V = 512, 2048, 1024, 512, 128, 512
FLOPS = 2 * K * H * S + 2 * H * N * V

F32 = mybir.dt.float32
BF16 = mybir.dt.bfloat16
I32 = mybir.dt.int32
U32 = mybir.dt.uint32
U16 = mybir.dt.uint16
U8 = mybir.dt.uint8
FP8X4 = mybir.dt.float8_e4m3fn_x4
MAX = mybir.AluOpType.max
MULT = mybir.AluOpType.mult
ADD = mybir.AluOpType.add

P = 128
PACK = 4
PIECE = 256
BLOCK = 128
HALF = 64
RUN = 4


def tile_picked_phpool_none_p_kernel(tc, x_words, x_scales, w1, w2, offs, out):
    nc = tc.nc
    with ExitStack() as ctx:
        keep = ctx.enter_context(tc.tile_pool(name="keep", bufs=1))
        ring = ctx.enter_context(tc.tile_pool(name="ring", bufs=4))
        psum = ctx.enter_context(tc.psum_pool(name="psum", bufs=1))

        w1_rows = w1.rearrange("(p j) c -> p j c", j=PACK)
        w1_raw = keep.tile([P, PACK, H], F32, name="w1_raw")
        nc.sync.dma_start(w1_raw[:, 0, :], w1_rows[:, 0, :])

        offsets = keep.tile([P, S // 16], U16, name="offsets")
        nc.sync.dma_start(offsets[:], offs)

        scale_table = keep.tile([P, T], U8, name="scale_table", tag="scales_then_w2", align_bytes=64)
        nc.vector.memset(scale_table[:].bitcast(I32), 0)
        x_plane = keep.tile([P, S], U8, name="x_plane", align_bytes=64)
        nc.vector.memset(x_plane[:].bitcast(I32), 0)

        word_table = keep.tile([P, T], I32, name="word_table", tag="words_then_w2", align_bytes=64)

        nc.sync.dma_start(scale_table[0:P:8, :].bitcast(I32), x_scales[0].bitcast(I32))
        nc.sync.dma_start(w1_raw[:, 1:PACK, :], w1_rows[:, 1:PACK, :])
        nc.sync.dma_start(word_table[:], x_words[0].rearrange("p n t -> p (n t)").bitcast(I32))

        picked_scales = keep.tile([P, S], U8, name="picked_scales", align_bytes=64)
        nc.vector.tensor_copy(picked_scales[:], scale_table[:].indirect(offsets[:]))
        for j in range(4):
            nc.sync.dma_start(
                x_plane[j:P:32, :].bitcast(I32), picked_scales[8 * j : P : 32, :].bitcast(I32)
            )
        w2_raw = keep.tile([P, PACK, N], F32, name="w2_raw", tag="scales_then_w2", align_bytes=64)
        w2_rows = w2.rearrange("(a t r) n -> r a t n", t=PACK, r=RUN)
        for r in range(RUN):
            nc.sync.dma_start(w2_raw[r:P:RUN], w2_rows[r])

        w1_by_tile = w1_raw[:].rearrange("p j (a t r) -> p t a j r", t=PACK, r=RUN)
        w1_codes = keep.tile([P, PACK, P], U32, name="w1_codes", align_bytes=64)
        w1_plane = keep.tile([P, PACK, P], U8, name="w1_plane", align_bytes=64)

        rounded = [keep.tile([P, P, PACK], BF16, name="w1_bf", tag="w1_bf%d" % t, align_bytes=64) for t in range(PACK)]

        def round_w1(round_copy, t, rows):
            round_copy(
                rounded[t][:].rearrange("p (a r) j -> p a j r", r=RUN)[:, :, rows], w1_by_tile[:, t, :, rows]
            )

        def quantise_w1(t):
            nc.vector.quantize_mx(
                out=w1_codes[:, t].bitcast(FP8X4),
                scales=w1_plane[:, t],
                in_=rounded[t][:].rearrange("p m j -> p (m j)"),
            )

        late_rows = slice(1, PACK)
        for t in range(2):
            round_w1(nc.scalar.copy, t, slice(0, 1))
        for t in range(2):
            round_w1(nc.scalar.copy, t, late_rows)
        for t in range(2, PACK):
            round_w1(nc.vector.tensor_copy, t, slice(0, PACK))
        for t in (2, 3, 0, 1):
            quantise_w1(t)

        all_codes = w1_codes[:].rearrange("p t m -> p (t m)").bitcast(FP8X4)
        all_planes = w1_plane[:].rearrange("p t m -> p (t m)")
        warm_bank = psum.tile([P, H], F32, name="warm_bank", tag="bank%d" % (S - BLOCK))
        for first, width in ((2 * P, P), (2 * P, P), (2 * P, P), (2 * P, P), (0, H)):
            nc.tensor.matmul_mx(
                out=warm_bank[:32, :width],
                lhsT=all_codes[:, 2 * P : 2 * P + 32],
                lhsT_scale=all_planes[:, 2 * P : 2 * P + 32],
                rhs=all_codes[:, first : first + width],
                rhs_scale=all_planes[:, first : first + width],
                start=True,
                stop=True,
            )

        picked_words = {}
        for half in range(V // PIECE):
            for read in range(2):
                first = read * V + half * PIECE
                words = keep.tile([P, PIECE], U32, name="words", tag="words%d" % first, align_bytes=64)[:]
                nc.vector.tensor_copy(
                    words,
                    word_table[:].bitcast(U32).indirect(offsets[:, first // 16 : (first + PIECE) // 16]),
                )
                picked_words[first] = words

        w2_and_z = keep.tile([P, N + BLOCK, PACK], BF16, name="w2_and_z", tag="words_then_w2", align_bytes=64)
        nc.gpsimd.tensor_scalar(w2_and_z[:, :N, :], w2_raw[:].rearrange("p j n -> p n j"), 1.0, 0.0, MULT, ADD)

        def project(bank, first):
            words = picked_words[first // PIECE * PIECE]
            inside = first % PIECE
            for t in range(PACK):
                nc.tensor.matmul_mx(
                    out=bank[:, t, :],
                    lhsT=w1_codes[:, t, :].bitcast(FP8X4),
                    lhsT_scale=w1_plane[:, t, :],
                    rhs=words[:, inside : inside + BLOCK].bitcast(FP8X4),
                    rhs_scale=x_plane[:, first : first + BLOCK],
                    start=True,
                    stop=True,
                )

        def quantise(values, tag):
            width = values.shape[1]
            codes = keep.tile([P, width], U32, name="codes", tag=tag, align_bytes=64)
            plane = keep.tile([P, width], U8, name="plane", tag=tag + "_plane", align_bytes=64)
            nc.vector.quantize_mx(
                out=codes[:].bitcast(FP8X4), scales=plane[:], in_=values.rearrange("p v t -> p (v t)")
            )
            return codes[:], plane[:]

        def second_layer(v0, parts, copy_out):
            width = sum(z_codes.shape[1] for z_codes, z_plane in parts)
            bank_o = psum.tile([P, width], F32, name="bank_o", tag="bank%d" % (v0 if v0 % BLOCK == 0 else V))
            column = 0
            for z_codes, z_plane in parts:
                nc.tensor.matmul_mx(
                    out=bank_o[:, column : column + z_codes.shape[1]],
                    lhsT=w2_codes.bitcast(FP8X4),
                    lhsT_scale=w2_plane,
                    rhs=z_codes.bitcast(FP8X4),
                    rhs_scale=z_plane,
                    start=True,
                    stop=True,
                )
                column = column + z_codes.shape[1]
            result = keep.tile([P, width], F32, name="result", tag="result%d" % v0)
            copy_out(result[:], bank_o[:])
            nc.sync.dma_start(out[:, v0 : v0 + width], result[:])

        banks = {}
        order = [0]
        for v0 in range(0, V, BLOCK):
            if v0 + BLOCK < V:
                order.append(v0 + BLOCK)
            order.append(V + v0)
        for first in order:
            bank = psum.tile([P, PACK, BLOCK], F32, name="bank", tag="bank%d" % first)
            project(bank, first)
            banks[first] = bank[:].rearrange("p t v -> p v t")

        last = V - BLOCK
        staged = {}
        for v0 in range(0, last, BLOCK):
            first_read = ring.tile([P, BLOCK, PACK], F32, name="first_read")
            nc.scalar.copy(first_read[:], banks[v0])
            staged[v0] = first_read
        last_reads = keep.tile([P, 2, BLOCK, PACK], BF16, name="last_reads", align_bytes=64)
        nc.scalar.copy(last_reads[:, 0], banks[last])
        for h in range(0, BLOCK, HALF):
            nc.scalar.copy(last_reads[:, 1, h : h + HALF], banks[V + last][:, h : h + HALF])

        z_rest = keep.tile([P, 3, BLOCK, PACK], BF16, name="z_rest", align_bytes=64)
        z_of = {0: z_rest[:, 0], BLOCK: w2_and_z[:, N:, :], PIECE: z_rest[:, 1], last: z_rest[:, 2]}
        for v0 in range(0, PIECE, BLOCK):
            nc.vector.tensor_tensor(z_of[v0], banks[V + v0], staged[v0][:], MAX)
        first_z = quantise(z_of[0], "words%d" % PIECE)
        both_codes, both_plane = quantise(w2_and_z[:], "codes_both")
        w2_codes, w2_plane = both_codes[:, :N], both_plane[:, :N]
        second_layer(0, [first_z, (both_codes[:, N:], both_plane[:, N:])], nc.scalar.copy)
        nc.vector.tensor_tensor(z_of[PIECE], banks[V + PIECE], staged[PIECE][:], MAX)
        early, late = slice(0, HALF), slice(HALF, BLOCK)
        nc.vector.tensor_tensor(z_of[last][:, early], last_reads[:, 0, early], last_reads[:, 1, early], MAX)
        second_layer(PIECE, [quantise(z_of[PIECE], "codes_third")], nc.scalar.copy)
        nc.vector.tensor_tensor(z_of[last][:, late], last_reads[:, 0, late], last_reads[:, 1, late], MAX)
        halves = [quantise(z_of[last][:, early], "codes_early"), quantise(z_of[last][:, late], "codes_late")]
        second_layer(last, halves, nc.vector.tensor_copy)
